import numpy as np
import ml_dtypes


def mxq(x, axis, fmt="e4m3"):
    dtype, down = {"e4m3": (ml_dtypes.float8_e4m3fn, 7), "e5m2": (ml_dtypes.float8_e5m2, 14)}[fmt]
    v = np.moveaxis(np.asarray(x, np.float32).astype(ml_dtypes.bfloat16).astype(np.float64), axis, -1)
    blocks = v.reshape(v.shape[:-1] + (-1, 32))
    amax = np.abs(blocks).max(-1, keepdims=True)
    byte = np.maximum(np.where(amax > 0, np.frexp(amax)[1] - 1 + 127, 0) - down, 1)
    scale = np.exp2(byte - 127.0)
    codes = (blocks / scale).astype(np.float32).astype(dtype).astype(np.float64)
    return np.moveaxis((codes * scale).reshape(v.shape), -1, axis)


WIDE = False


def mx_kscale(k):
    if not WIDE:
        return np.ones(k)
    levels = np.array([10, -10, 5, -5, 0])
    if k % 512:
        return np.exp2(np.random.permutation(np.resize(levels, k // 32))).repeat(32)
    a = np.empty((k // 512, 16))
    for p in range(k // 512):
        a[p, :8] = np.random.permutation(np.resize(levels, 8))
        for g in range(8):
            far = levels[np.abs(levels - a[p, g]) >= 10]
            a[p, g + 8] = far[np.random.randint(len(far))]
    return np.exp2(a.ravel()).repeat(32)


def f64(x):
    return np.asarray(x).astype(np.float64)


def striped(idx):
    return np.tile(idx.reshape(-1, 16).T, (8, 1)).astype(np.uint16)


def unstriped(offs):
    return offs[:16].T.reshape(-1).astype(np.int64)


def pack_weight(w):
    k, n = w.shape
    w = f64(np.asarray(w, np.float32).astype(ml_dtypes.bfloat16)).reshape(k // 32, 32, n)
    amax = np.abs(w).max(1)
    byte = np.clip(np.where(amax > 0, np.frexp(amax)[1] - 1 + 127 - 7, 1), 1, 254)
    scaled = (w * np.exp2(127.0 - byte)[:, None, :]).reshape(k, n).astype(np.float32)
    words = np.ascontiguousarray(scaled.reshape(k // 512, 128, 4, n).transpose(0, 1, 3, 2)).astype(ml_dtypes.float8_e4m3fn).view(np.uint8)
    return words, np.ascontiguousarray(byte.astype(np.uint8).reshape(k // 512, 16, n))


def unpack_weight(words, scales):
    g, p, n, _ = words.shape
    vals = np.ascontiguousarray(words).view(ml_dtypes.float8_e4m3fn).astype(np.float64) * np.repeat(np.exp2(scales.astype(np.float64) - 127.0), 8, axis=1)[..., None]
    return vals.transpose(0, 1, 3, 2).reshape(g * 512, n)


def sigmoid(v):
    return 1.0 / (1.0 + np.exp(-np.maximum(v, -700.0)))


K, T, S, H, V, W, G, U = 512, 1024, 512, 512, 256, 1024, 1024, 512
P = 2 ** 7


def setup_inputs():
    n = np.random.standard_normal
    s = mx_kscale(K)[:, None]
    u = mx_kscale(H)
    packed_xT = pack_weight(n((K, T)) * s)
    packed_eT = pack_weight(n((H, W)) / np.sqrt(H) / u[:, None])
    packed_dT = pack_weight(n((H, G)) / np.sqrt(H) / u[:, None])
    return {
        "x_words": packed_xT[0],
        "x_scales": packed_xT[1],
        "w1": (n((K, H)) / np.sqrt(K) / s * u).astype(np.float32),
        "e_words": packed_eT[0],
        "e_scales": packed_eT[1],
        "d_words": packed_dT[0],
        "d_scales": packed_dT[1],
        "ms": (np.tile(0.3 * n(G), (P, 1))).astype(np.float32),
        "offs": striped(np.random.permutation(T)[:S]),
        "coh": striped(np.random.permutation(W)[:U]),
        "spk": striped(np.random.permutation(G)[:V]),
    }


def reference(x_words, x_scales, w1, e_words, e_scales, d_words, d_scales, ms, offs, coh, spk):
    xq = unpack_weight(x_words, x_scales)[:, unstriped(offs)]
    h = mxq(f64(w1), 0, "e4m3").T @ xq
    hq = mxq(h, 0, "e4m3")
    d_spk = unpack_weight(d_words, d_scales)[:, unstriped(spk)]
    y = hq.T @ d_spk
    e_coh = unpack_weight(e_words, e_scales)[:, unstriped(coh)]
    z = hq.T @ e_coh
    mean = z.mean(axis=1, keepdims=True)
    dz = z - mean
    d2 = (dz) ** 2
    sd = np.sqrt(d2.mean(axis=1, keepdims=True) + 0.01)
    nz = (y - mean) / sd
    return sigmoid(2.0 * nz - (f64(ms)[:1][:, unstriped(spk)]))

@@ -1,0 +1,210 @@
+from contextlib import ExitStack
+
+import concourse.mybir as mybir
+
+F32 = mybir.dt.float32
+BF16 = mybir.dt.bfloat16
+I32 = mybir.dt.int32
+U32 = mybir.dt.uint32
+U16 = mybir.dt.uint16
+U8 = mybir.dt.uint8
+FP8X4 = mybir.dt.float8_e4m3fn_x4
+ALU = mybir.AluOpType
+ACT = mybir.ActivationFunctionType
+
+P = 128
+PACK = 4
+STORE = 1024
+S, H, U, V = 512, 512, 512, 256
+TILES = S // P
+EPS = 0.01
+SCALAR_STATS = 2
+
+FLOPS = 2 * 512 * H * S + 2 * H * S * (U + V)
+
+
+def tile_picked_ysnorm_cal_p_kernel(tc, x_words, x_scales, w1, e_words, e_scales, d_words, d_scales, ms, offs, coh, spk, out):
+    nc = tc.nc
+    with ExitStack() as ctx:
+        keep = ctx.enter_context(tc.tile_pool(name="keep", bufs=1))
+        psum = ctx.enter_context(tc.psum_pool(name="psum", bufs=1))
+
+        def sb(shape, dtype, name):
+            return keep.tile(shape, dtype, name=name, align_bytes=64)
+
+        def load_words(words, name):
+            table = sb([P, STORE], U32, name)
+            nc.sync.dma_start(table[:].bitcast(I32), words[0].rearrange("p n t -> p (n t)").bitcast(I32))
+            return table
+
+        def load_scales(scales, name, repeat, queue):
+            table = sb([P, STORE], U8, name)
+            rows = scales[0].bitcast(I32)
+            if not repeat:
+                nc.gpsimd.memset(table[:].bitcast(I32), 0)
+            for q in range(4):
+                if repeat:
+                    src = rows[4 * q : 4 * q + 4, :].unsqueeze(0).to_broadcast([8, 4, STORE // 4])
+                    queue.dma_start(table[32 * q : 32 * q + 32, :].bitcast(I32), src)
+                else:
+                    queue.dma_start(table[32 * q : 32 * q + 4, :].bitcast(I32), rows[4 * q : 4 * q + 4, :])
+            return table
+
+        def load_list(lst, n, name):
+            tile = sb([P, n // 16], U16, name)
+            nc.sync.dma_start(tile[:], lst)
+            return tile
+
+        w_rows = w1.rearrange("(p j) c -> p j c", j=PACK)
+
+        def load_w(u):
+            raw = sb([P, PACK, H // 2], F32, "w_raw%d" % u)
+            nc.sync.dma_start(raw[:], w_rows[:, :, u * (H // 2) : (u + 1) * (H // 2)])
+            return raw
+
+        w_raw = [load_w(0)]
+        offs_sb = load_list(offs, S, "offs_sb")
+        xs_tab = load_scales(x_scales, "xs_tab", True, nc.sync)
+        xw_tab = load_words(x_words, "xw_tab")
+        w_raw.append(load_w(1))
+        coh_sb = load_list(coh, U, "coh_sb")
+        es_tab = load_scales(e_scales, "es_tab", False, nc.sync)
+        ew_tab = load_words(e_words, "ew_tab")
+        spk_sb = load_list(spk, V, "spk_sb")
+        ds_tab = load_scales(d_scales, "ds_tab", False, nc.sync)
+        dw_tab = load_words(d_words, "dw_tab")
+        ms_tab = sb([P, STORE], F32, "ms_tab")
+        nc.sync.dma_start(ms_tab[:], ms)
+
+        half = sb([P, 1], F32, "minus_half")
+        nc.gpsimd.memset(half[:], -0.5)
+        warm = sb([P, 1], F32, "warm")
+        nc.scalar.activation(warm[:], half[:], ACT.Sigmoid)
+
+        xs = sb([P, S], U8, "xs")
+        nc.vector.tensor_copy(xs[:], xs_tab[:].indirect(offs_sb[:]))
+
+        xw = sb([P, S], U32, "xw")
+        for c in range(TILES):
+            nc.vector.tensor_copy(xw[:, P * c : P * (c + 1)], xw_tab[:].indirect(offs_sb[:, 8 * c : 8 * (c + 1)]))
+
+        w_bf = sb([P, PACK, P, PACK], BF16, "w_bf")
+        w_codes = sb([P, H], U32, "w_codes")
+        w_scales = sb([P, H], U8, "w_scales")
+        es = sb([P, U], U8, "es")
+        for u in range(2):
+            ms_ = slice(64 * u, 64 * (u + 1))
+            nc.scalar.copy(
+                w_bf[:, :, ms_, :].rearrange("p t m j -> p m j t"),
+                w_raw[u][:].rearrange("p j (m t) -> p m j t", t=PACK),
+            )
+            for t in range(PACK):
+                cols = slice(P * t + 64 * u, P * t + 64 * (u + 1))
+                nc.vector.quantize_mx(
+                    out=w_codes[:, cols].bitcast(FP8X4),
+                    scales=w_scales[:, cols],
+                    in_=w_bf[:, t, ms_, :].rearrange("p m j -> p (m j)"),
+                )
+            if u == 0:
+                nc.vector.tensor_copy(es[:], es_tab[:].indirect(coh_sb[:]))
+
+        banks = ["bank%d" % b for b in range(8)]
+        h_bf = []
+        for c in range(TILES):
+            tok = slice(P * c, P * (c + 1))
+            h_ps = psum.tile([P, PACK, P], F32, name="h_ps%d" % c, tag=banks[c])
+            for t in range(PACK):
+                cols = slice(P * t, P * (t + 1))
+                nc.tensor.matmul_mx(
+                    out=h_ps[:, t, :],
+                    lhsT=w_codes[:, cols].bitcast(FP8X4),
+                    lhsT_scale=w_scales[:, cols],
+                    rhs=xw[:, tok].bitcast(FP8X4),
+                    rhs_scale=xs[:, tok],
+                    start=True,
+                    stop=True,
+                )
+            hb = sb([P, P, PACK], BF16, "h_bf%d" % c)
+            nc.scalar.copy(hb[:], h_ps[:].rearrange("p t n -> p n t"))
+            h_bf.append(hb)
+
+        ew = sb([P, U], U32, "ew")
+        nc.vector.tensor_copy(ew[:], ew_tab[:].indirect(coh_sb[:]))
+        ds = sb([P, V], U8, "ds")
+        dw = sb([P, V], U32, "dw")
+        ms_spk = sb([P, V], F32, "ms_spk")
+
+        h_codes = sb([P, S], U32, "h_codes")
+        h_scales = sb([P, S], U8, "h_scales")
+        z_ps, y_ps = [], []
+        for c in range(TILES):
+            tok = slice(P * c, P * (c + 1))
+            nc.vector.quantize_mx(
+                out=h_codes[:, tok].bitcast(FP8X4),
+                scales=h_scales[:, tok],
+                in_=h_bf[c][:].rearrange("p n t -> p (n t)"),
+            )
+            z = psum.tile([P, U], F32, name="z_ps%d" % c, tag=banks[(4 + 2 * c) % 8])
+            nc.tensor.matmul_mx(
+                out=z[:],
+                lhsT=h_codes[:, tok].bitcast(FP8X4),
+                lhsT_scale=h_scales[:, tok],
+                rhs=ew[:].bitcast(FP8X4),
+                rhs_scale=es[:],
+                start=True,
+                stop=True,
+            )
+            z_ps.append(z)
+            if c == 0:
+                nc.vector.tensor_copy(ds[:], ds_tab[:].indirect(spk_sb[:]))
+                nc.vector.tensor_copy(dw[:], dw_tab[:].indirect(spk_sb[:]))
+        nc.vector.tensor_copy(ms_spk[:], ms_tab[:].indirect(spk_sb[:]))
+        for c in range(TILES):
+            tok = slice(P * c, P * (c + 1))
+            y = psum.tile([P, V], F32, name="y_ps%d" % c, tag=banks[(5 + 2 * c) % 8])
+            nc.tensor.matmul_mx(
+                out=y[:],
+                lhsT=h_codes[:, tok].bitcast(FP8X4),
+                lhsT_scale=h_scales[:, tok],
+                rhs=dw[:].bitcast(FP8X4),
+                rhs_scale=ds[:],
+                start=True,
+                stop=True,
+            )
+            y_ps.append(y)
+
+        gains, shifts = [], []
+        spill = sb([P, U], BF16, "spill")
+        neg_means, squares = [], []
+        for c in range(SCALAR_STATS):
+            neg_mean = sb([P, 1], F32, "neg_mean%d" % c)
+            nc.scalar.activation(spill[:], z_ps[c][:], ACT.Copy, scale=-1.0 / U, accum_out=neg_mean[:])
+            neg_means.append(neg_mean)
+        for c in range(SCALAR_STATS):
+            square = sb([P, 1], F32, "square%d" % c)
+            nc.scalar.activation(spill[:], z_ps[c][:], ACT.Square, bias=neg_means[c][:], accum_out=square[:])
+            squares.append(square)
+        for c in range(TILES):
+            if c < SCALAR_STATS:
+                mean, sign, spread, count = neg_means[c][:], 1.0, squares[c][:], U
+            else:
+                stats = sb([P, 6], F32, "stats%d" % c)
+                nc.vector.bn_stats(stats[:], z_ps[c][:])
+                mean_var = sb([P, 2], F32, "mean_var%d" % c)
+                nc.vector.bn_aggr(mean_var[:], stats[:])
+                mean, sign, spread, count = mean_var[:, 0:1], -1.0, mean_var[:, 1:2], 1
+            quarter = sb([P, 1], F32, "quarter%d" % c)
+            nc.gpsimd.tensor_scalar(quarter[:], spread, 0.25 / count, 0.25 * EPS, ALU.mult, ALU.add)
+            gain = sb([P, 1], F32, "gain%d" % c)
+            nc.gpsimd.tensor_tensor(gain[:], quarter[:], half[:], ALU.pow)
+            shift = sb([P, 1], F32, "shift%d" % c)
+            nc.gpsimd.tensor_scalar(shift[:], mean, gain[:], sign, ALU.mult, ALU.mult)
+            gains.append(gain)
+            shifts.append(shift)
+        for c in range(TILES):
+            tok = slice(P * c, P * (c + 1))
+            logit = sb([P, V], F32, "logit%d" % c)
+            nc.vector.scalar_tensor_tensor(logit[:], y_ps[c][:], gains[c][:], ms_spk[:], ALU.mult, ALU.subtract)
+            prob = sb([P, V], F32, "prob%d" % c)
+            nc.scalar.activation(prob[:], logit[:], ACT.Sigmoid, bias=shifts[c][:])
+            nc.sync.dma_start(out[tok, :], prob[:])

@@ -18,7 +18,9 @@ STORE = 1024
 S, H, U, V = 512, 512, 512, 256
 TILES = S // P
 EPS = 0.01
-SCALAR_STATS = 2
+HALF_M = P // 2
+LAST = 1
+SCALAR_M = 40
 
 FLOPS = 2 * 512 * H * S + 2 * H * S * (U + V)
 
@@ -29,31 +31,26 @@ def tile_picked_ysnorm_cal_p_kernel(tc, x_words, x_scales, w1, e_words, e_scales
         keep = ctx.enter_context(tc.tile_pool(name="keep", bufs=1))
         psum = ctx.enter_context(tc.psum_pool(name="psum", bufs=1))
 
-        def sb(shape, dtype, name):
-            return keep.tile(shape, dtype, name=name, align_bytes=64)
+        def sb(shape, dtype, name, slot=""):
+            return keep.tile(shape, dtype, name=name, tag=slot or name, align_bytes=64)
 
         def load_words(words, name):
             table = sb([P, STORE], U32, name)
             nc.sync.dma_start(table[:].bitcast(I32), words[0].rearrange("p n t -> p (n t)").bitcast(I32))
             return table
 
-        def load_scales(scales, name, repeat, queue):
+        def load_scales(scales, name):
             table = sb([P, STORE], U8, name)
             rows = scales[0].bitcast(I32)
-            if not repeat:
-                nc.gpsimd.memset(table[:].bitcast(I32), 0)
+            nc.gpsimd.memset(table[:].bitcast(I32), 0)
             for q in range(4):
-                if repeat:
-                    src = rows[4 * q : 4 * q + 4, :].unsqueeze(0).to_broadcast([8, 4, STORE // 4])
-                    queue.dma_start(table[32 * q : 32 * q + 32, :].bitcast(I32), src)
-                else:
-                    queue.dma_start(table[32 * q : 32 * q + 4, :].bitcast(I32), rows[4 * q : 4 * q + 4, :])
+                nc.sync.dma_start(table[32 * q : 32 * q + 4, :].bitcast(I32), rows[4 * q : 4 * q + 4, :])
             return table
 
         def load_list(lst, n, name):
-            tile = sb([P, n // 16], U16, name)
-            nc.sync.dma_start(tile[:], lst)
-            return tile
+            offsets = sb([P, n // 16], U16, name)
+            nc.sync.dma_start(offsets[:], lst)
+            return offsets
 
         w_rows = w1.rearrange("(p j) c -> p j c", j=PACK)
 
@@ -62,149 +59,129 @@ def tile_picked_ysnorm_cal_p_kernel(tc, x_words, x_scales, w1, e_words, e_scales
             nc.sync.dma_start(raw[:], w_rows[:, :, u * (H // 2) : (u + 1) * (H // 2)])
             return raw
 
-        w_raw = [load_w(0)]
-        offs_sb = load_list(offs, S, "offs_sb")
-        xs_tab = load_scales(x_scales, "xs_tab", True, nc.sync)
         xw_tab = load_words(x_words, "xw_tab")
-        w_raw.append(load_w(1))
+        offs_sb = load_list(offs, S, "offs_sb")
+        xs_tab = load_scales(x_scales, "xs_tab")
+        w_raw = [load_w(0), load_w(1)]
         coh_sb = load_list(coh, U, "coh_sb")
-        es_tab = load_scales(e_scales, "es_tab", False, nc.sync)
+        es_tab = load_scales(e_scales, "es_tab")
         ew_tab = load_words(e_words, "ew_tab")
-        spk_sb = load_list(spk, V, "spk_sb")
-        ds_tab = load_scales(d_scales, "ds_tab", False, nc.sync)
         dw_tab = load_words(d_words, "dw_tab")
+        spk_sb = load_list(spk, V, "spk_sb")
+        ds_tab = load_scales(d_scales, "ds_tab")
         ms_tab = sb([P, STORE], F32, "ms_tab")
         nc.sync.dma_start(ms_tab[:], ms)
 
-        half = sb([P, 1], F32, "minus_half")
-        nc.gpsimd.memset(half[:], -0.5)
-        warm = sb([P, 1], F32, "warm")
-        nc.scalar.activation(warm[:], half[:], ACT.Sigmoid)
+        zero = sb([P, 2], F32, "zero")
+        nc.vector.memset(zero[:], 0.0)
+        half = sb([P, 2], F32, "half")
+        nc.scalar.activation(half[:], zero[:], ACT.Sigmoid)
+        minus_half = sb([P, 2], F32, "minus_half")
+        nc.scalar.activation(minus_half[:], half[:], ACT.Copy, scale=-1.0)
 
-        xs = sb([P, S], U8, "xs")
-        nc.vector.tensor_copy(xs[:], xs_tab[:].indirect(offs_sb[:]))
+        def gather(table, offsets, n, dtype, name, slot=""):
+            picked = sb([P, n], dtype, name, slot)
+            nc.vector.tensor_copy(picked[:], table[:].indirect(offsets[:]))
+            return picked
 
-        xw = sb([P, S], U32, "xw")
-        for c in range(TILES):
-            nc.vector.tensor_copy(xw[:, P * c : P * (c + 1)], xw_tab[:].indirect(offs_sb[:, 8 * c : 8 * (c + 1)]))
+        xw = gather(xw_tab, offs_sb, S, U32, "xw")
+        xs = gather(xs_tab, offs_sb, S, U8, "xs")
 
         w_bf = sb([P, PACK, P, PACK], BF16, "w_bf")
         w_codes = sb([P, H], U32, "w_codes")
         w_scales = sb([P, H], U8, "w_scales")
-        es = sb([P, U], U8, "es")
         for u in range(2):
-            ms_ = slice(64 * u, 64 * (u + 1))
-            nc.scalar.copy(
-                w_bf[:, :, ms_, :].rearrange("p t m j -> p m j t"),
-                w_raw[u][:].rearrange("p j (m t) -> p m j t", t=PACK),
-            )
+            dealt = w_bf[:, :, HALF_M * u : HALF_M * (u + 1), :].rearrange("p t m j -> p m j t")
+            rows = w_raw[u][:].rearrange("p j (m t) -> p m j t", t=PACK)
+            if u == 0:
+                nc.scalar.copy(dealt, rows)
+            else:
+                nc.scalar.copy(dealt[:, :SCALAR_M], rows[:, :SCALAR_M])
+                nc.vector.tensor_copy(dealt[:, SCALAR_M:], rows[:, SCALAR_M:])
             for t in range(PACK):
-                cols = slice(P * t + 64 * u, P * t + 64 * (u + 1))
+                cols = slice(P * t + HALF_M * u, P * t + HALF_M * (u + 1))
                 nc.vector.quantize_mx(
                     out=w_codes[:, cols].bitcast(FP8X4),
                     scales=w_scales[:, cols],
-                    in_=w_bf[:, t, ms_, :].rearrange("p m j -> p (m j)"),
+                    in_=w_bf[:, t, HALF_M * u : HALF_M * (u + 1), :].rearrange("p m j -> p (m j)"),
                 )
-            if u == 0:
-                nc.vector.tensor_copy(es[:], es_tab[:].indirect(coh_sb[:]))
 
-        banks = ["bank%d" % b for b in range(8)]
+        def product(acc, lhs_codes, lhs_scales, rhs_codes, rhs_scales):
+            nc.tensor.matmul_mx(
+                out=acc,
+                lhsT=lhs_codes.bitcast(FP8X4),
+                lhsT_scale=lhs_scales,
+                rhs=rhs_codes.bitcast(FP8X4),
+                rhs_scale=rhs_scales,
+                start=True,
+                stop=True,
+            )
+
         h_bf = []
         for c in range(TILES):
             tok = slice(P * c, P * (c + 1))
-            h_ps = psum.tile([P, PACK, P], F32, name="h_ps%d" % c, tag=banks[c])
+            h_ps = psum.tile([P, PACK, P], F32, name="h_ps%d" % c, tag="bank%d" % c)
             for t in range(PACK):
                 cols = slice(P * t, P * (t + 1))
-                nc.tensor.matmul_mx(
-                    out=h_ps[:, t, :],
-                    lhsT=w_codes[:, cols].bitcast(FP8X4),
-                    lhsT_scale=w_scales[:, cols],
-                    rhs=xw[:, tok].bitcast(FP8X4),
-                    rhs_scale=xs[:, tok],
-                    start=True,
-                    stop=True,
-                )
-            hb = sb([P, P, PACK], BF16, "h_bf%d" % c)
-            nc.scalar.copy(hb[:], h_ps[:].rearrange("p t n -> p n t"))
-            h_bf.append(hb)
+                product(h_ps[:, t, :], w_codes[:, cols], w_scales[:, cols], xw[:, tok], xs[:, tok])
+            rounded = sb([P, P, PACK], BF16, "h_bf%d" % c)
+            nc.scalar.copy(rounded[:], h_ps[:].rearrange("p t n -> p n t"))
+            h_bf.append(rounded)
 
-        ew = sb([P, U], U32, "ew")
-        nc.vector.tensor_copy(ew[:], ew_tab[:].indirect(coh_sb[:]))
-        ds = sb([P, V], U8, "ds")
-        dw = sb([P, V], U32, "dw")
-        ms_spk = sb([P, V], F32, "ms_spk")
+        es = gather(es_tab, coh_sb, U, U8, "es")
+        ew = gather(ew_tab, coh_sb, U, U32, "ew")
 
-        h_codes = sb([P, S], U32, "h_codes")
+        h_codes = sb([P, S], U32, "h_codes", "ew_tab")
         h_scales = sb([P, S], U8, "h_scales")
-        z_ps, y_ps = [], []
+        z_ps = []
         for c in range(TILES):
             tok = slice(P * c, P * (c + 1))
-            nc.vector.quantize_mx(
-                out=h_codes[:, tok].bitcast(FP8X4),
-                scales=h_scales[:, tok],
-                in_=h_bf[c][:].rearrange("p n t -> p (n t)"),
-            )
-            z = psum.tile([P, U], F32, name="z_ps%d" % c, tag=banks[(4 + 2 * c) % 8])
-            nc.tensor.matmul_mx(
-                out=z[:],
-                lhsT=h_codes[:, tok].bitcast(FP8X4),
-                lhsT_scale=h_scales[:, tok],
-                rhs=ew[:].bitcast(FP8X4),
-                rhs_scale=es[:],
-                start=True,
-                stop=True,
-            )
+            nc.vector.quantize_mx(out=h_codes[:, tok].bitcast(FP8X4), scales=h_scales[:, tok], in_=h_bf[c][:].rearrange("p n t -> p (n t)"))
+            z = psum.tile([P, U], F32, name="z_ps%d" % c, tag="bank%d" % (TILES + c))
+            product(z[:], h_codes[:, tok], h_scales[:, tok], ew[:], es[:])
             z_ps.append(z)
-            if c == 0:
-                nc.vector.tensor_copy(ds[:], ds_tab[:].indirect(spk_sb[:]))
-                nc.vector.tensor_copy(dw[:], dw_tab[:].indirect(spk_sb[:]))
-        nc.vector.tensor_copy(ms_spk[:], ms_tab[:].indirect(spk_sb[:]))
-        for c in range(TILES):
-            tok = slice(P * c, P * (c + 1))
-            y = psum.tile([P, V], F32, name="y_ps%d" % c, tag=banks[(5 + 2 * c) % 8])
-            nc.tensor.matmul_mx(
-                out=y[:],
-                lhsT=h_codes[:, tok].bitcast(FP8X4),
-                lhsT_scale=h_scales[:, tok],
-                rhs=dw[:].bitcast(FP8X4),
-                rhs_scale=ds[:],
-                start=True,
-                stop=True,
-            )
-            y_ps.append(y)
 
-        gains, shifts = [], []
+        dw = gather(dw_tab, spk_sb, V, U32, "dw", "h_bf1")
+
+        neg_mean = sb([P, TILES], F32, "neg_mean")
+        gain = sb([P, TILES], F32, "gain")
+        shift = sb([P, TILES], F32, "shift")
         spill = sb([P, U], BF16, "spill")
-        neg_means, squares = [], []
-        for c in range(SCALAR_STATS):
-            neg_mean = sb([P, 1], F32, "neg_mean%d" % c)
-            nc.scalar.activation(spill[:], z_ps[c][:], ACT.Copy, scale=-1.0 / U, accum_out=neg_mean[:])
-            neg_means.append(neg_mean)
-        for c in range(SCALAR_STATS):
-            square = sb([P, 1], F32, "square%d" % c)
-            nc.scalar.activation(spill[:], z_ps[c][:], ACT.Square, bias=neg_means[c][:], accum_out=square[:])
-            squares.append(square)
-        for c in range(TILES):
-            if c < SCALAR_STATS:
-                mean, sign, spread, count = neg_means[c][:], 1.0, squares[c][:], U
-            else:
-                stats = sb([P, 6], F32, "stats%d" % c)
-                nc.vector.bn_stats(stats[:], z_ps[c][:])
-                mean_var = sb([P, 2], F32, "mean_var%d" % c)
-                nc.vector.bn_aggr(mean_var[:], stats[:])
-                mean, sign, spread, count = mean_var[:, 0:1], -1.0, mean_var[:, 1:2], 1
-            quarter = sb([P, 1], F32, "quarter%d" % c)
-            nc.gpsimd.tensor_scalar(quarter[:], spread, 0.25 / count, 0.25 * EPS, ALU.mult, ALU.add)
-            gain = sb([P, 1], F32, "gain%d" % c)
-            nc.gpsimd.tensor_tensor(gain[:], quarter[:], half[:], ALU.pow)
-            shift = sb([P, 1], F32, "shift%d" % c)
-            nc.gpsimd.tensor_scalar(shift[:], mean, gain[:], sign, ALU.mult, ALU.mult)
-            gains.append(gain)
-            shifts.append(shift)
-        for c in range(TILES):
+        squares = sb([P, 2], F32, "squares")
+        quarter = sb([P, 2], F32, "quarter")
+        for c in range(2):
+            own = slice(c, c + 1)
+            nc.scalar.activation(spill[:], z_ps[c][:], ACT.Copy, scale=-1.0 / U, accum_out=neg_mean[:, own])
+            nc.scalar.activation(spill[:], z_ps[c][:], ACT.Square, bias=neg_mean[:, own], accum_out=squares[:, own])
+            nc.scalar.activation(quarter[:, own], squares[:, own], ACT.Copy, scale=0.25 / U, bias=0.25 * EPS)
+        stats = sb([P, 2, 6], F32, "stats", "dw_tab")
+        mean_var = sb([P, 2, 2], F32, "mean_var")
+        for g in range(2):
+            nc.vector.bn_stats(stats[:, g, :], z_ps[2 + g][:])
+        for g in range(2):
+            nc.vector.bn_aggr(mean_var[:, g, :], stats[:, g, :])
+        quarter_late = sb([P, 2], F32, "quarter_late")
+        nc.scalar.activation(neg_mean[:, 2:4], mean_var[:, :, 0], ACT.Copy, scale=-1.0)
+
+        ds = gather(ds_tab, spk_sb, V, U8, "ds")
+        ms_spk = gather(ms_tab, spk_sb, V, F32, "ms_spk")
+
+        nc.gpsimd.tensor_tensor(gain[:, 0:1], quarter[:, 0:1], minus_half[:, 0:1], ALU.pow)
+        nc.gpsimd.tensor_scalar(quarter_late[:], mean_var[:, :, 1], 0.25, 0.25 * EPS, ALU.mult, ALU.add)
+        nc.gpsimd.tensor_tensor(gain[:, 2:4], quarter_late[:], minus_half[:], ALU.pow)
+        nc.gpsimd.tensor_tensor(gain[:, 1:2], quarter[:, 1:2], minus_half[:, 0:1], ALU.pow)
+
+        for c in (0, 2, 3, 1):
             tok = slice(P * c, P * (c + 1))
-            logit = sb([P, V], F32, "logit%d" % c)
-            nc.vector.scalar_tensor_tensor(logit[:], y_ps[c][:], gains[c][:], ms_spk[:], ALU.mult, ALU.subtract)
-            prob = sb([P, V], F32, "prob%d" % c)
-            nc.scalar.activation(prob[:], logit[:], ACT.Sigmoid, bias=shifts[c][:])
-            nc.sync.dma_start(out[tok, :], prob[:])
+            own = slice(c, c + 1)
+            y = psum.tile([P, V], F32, name="y_ps%d" % c, tag="bank%d" % c)
+            product(y[:], h_codes[:, tok], h_scales[:, tok], dw[:], ds[:])
+            nc.scalar.activation(shift[:, own], neg_mean[:, own], ACT.Copy, scale=gain[:, own])
+            pieces = 2 if c == LAST else 1
+            for k in range(pieces):
+                cols = slice(V // pieces * k, V // pieces * (k + 1))
+                logit = sb([P, V // pieces], F32, "logit%d_%d" % (c, k))
+                nc.vector.scalar_tensor_tensor(logit[:], y[:, cols], gain[:, own], ms_spk[:, cols], ALU.mult, ALU.subtract)
+                prob = sb([P, V // pieces], F32, "prob%d_%d" % (c, k))
+                nc.scalar.activation(prob[:], logit[:], ACT.Sigmoid, bias=shift[:, own])
+                nc.sync.dma_start(out[tok, cols], prob[:])

from contextlib import ExitStack

import concourse.mybir as mybir

F32 = mybir.dt.float32
BF16 = mybir.dt.bfloat16
I32 = mybir.dt.int32
U32 = mybir.dt.uint32
U16 = mybir.dt.uint16
U8 = mybir.dt.uint8
FP8X4 = mybir.dt.float8_e4m3fn_x4
ALU = mybir.AluOpType
ACT = mybir.ActivationFunctionType

P = 128
PACK = 4
STORE = 1024
S, H, U, V = 512, 512, 512, 256
TILES = S // P
EPS = 0.01
HALF_M = P // 2
LAST = 1
SCALAR_M = 40

FLOPS = 2 * 512 * H * S + 2 * H * S * (U + V)


def tile_picked_ysnorm_cal_p_kernel(tc, x_words, x_scales, w1, e_words, e_scales, d_words, d_scales, ms, offs, coh, spk, out):
    nc = tc.nc
    with ExitStack() as ctx:
        keep = ctx.enter_context(tc.tile_pool(name="keep", bufs=1))
        psum = ctx.enter_context(tc.psum_pool(name="psum", bufs=1))

        def sb(shape, dtype, name, slot=""):
            return keep.tile(shape, dtype, name=name, tag=slot or name, align_bytes=64)

        def load_words(words, name):
            table = sb([P, STORE], U32, name)
            nc.sync.dma_start(table[:].bitcast(I32), words[0].rearrange("p n t -> p (n t)").bitcast(I32))
            return table

        def load_scales(scales, name):
            table = sb([P, STORE], U8, name)
            rows = scales[0].bitcast(I32)
            nc.gpsimd.memset(table[:].bitcast(I32), 0)
            for q in range(4):
                nc.sync.dma_start(table[32 * q : 32 * q + 4, :].bitcast(I32), rows[4 * q : 4 * q + 4, :])
            return table

        def load_list(lst, n, name):
            offsets = sb([P, n // 16], U16, name)
            nc.sync.dma_start(offsets[:], lst)
            return offsets

        w_rows = w1.rearrange("(p j) c -> p j c", j=PACK)

        def load_w(u):
            raw = sb([P, PACK, H // 2], F32, "w_raw%d" % u)
            nc.sync.dma_start(raw[:], w_rows[:, :, u * (H // 2) : (u + 1) * (H // 2)])
            return raw

        xw_tab = load_words(x_words, "xw_tab")
        offs_sb = load_list(offs, S, "offs_sb")
        xs_tab = load_scales(x_scales, "xs_tab")
        w_raw = [load_w(0), load_w(1)]
        coh_sb = load_list(coh, U, "coh_sb")
        es_tab = load_scales(e_scales, "es_tab")
        ew_tab = load_words(e_words, "ew_tab")
        dw_tab = load_words(d_words, "dw_tab")
        spk_sb = load_list(spk, V, "spk_sb")
        ds_tab = load_scales(d_scales, "ds_tab")
        ms_tab = sb([P, STORE], F32, "ms_tab")
        nc.sync.dma_start(ms_tab[:], ms)

        zero = sb([P, 2], F32, "zero")
        nc.vector.memset(zero[:], 0.0)
        half = sb([P, 2], F32, "half")
        nc.scalar.activation(half[:], zero[:], ACT.Sigmoid)
        minus_half = sb([P, 2], F32, "minus_half")
        nc.scalar.activation(minus_half[:], half[:], ACT.Copy, scale=-1.0)

        def gather(table, offsets, n, dtype, name, slot=""):
            picked = sb([P, n], dtype, name, slot)
            nc.vector.tensor_copy(picked[:], table[:].indirect(offsets[:]))
            return picked

        xw = gather(xw_tab, offs_sb, S, U32, "xw")
        xs = gather(xs_tab, offs_sb, S, U8, "xs")

        w_bf = sb([P, PACK, P, PACK], BF16, "w_bf")
        w_codes = sb([P, H], U32, "w_codes")
        w_scales = sb([P, H], U8, "w_scales")
        for u in range(2):
            dealt = w_bf[:, :, HALF_M * u : HALF_M * (u + 1), :].rearrange("p t m j -> p m j t")
            rows = w_raw[u][:].rearrange("p j (m t) -> p m j t", t=PACK)
            if u == 0:
                nc.scalar.copy(dealt, rows)
            else:
                nc.scalar.copy(dealt[:, :SCALAR_M], rows[:, :SCALAR_M])
                nc.vector.tensor_copy(dealt[:, SCALAR_M:], rows[:, SCALAR_M:])
            for t in range(PACK):
                cols = slice(P * t + HALF_M * u, P * t + HALF_M * (u + 1))
                nc.vector.quantize_mx(
                    out=w_codes[:, cols].bitcast(FP8X4),
                    scales=w_scales[:, cols],
                    in_=w_bf[:, t, HALF_M * u : HALF_M * (u + 1), :].rearrange("p m j -> p (m j)"),
                )

        def product(acc, lhs_codes, lhs_scales, rhs_codes, rhs_scales):
            nc.tensor.matmul_mx(
                out=acc,
                lhsT=lhs_codes.bitcast(FP8X4),
                lhsT_scale=lhs_scales,
                rhs=rhs_codes.bitcast(FP8X4),
                rhs_scale=rhs_scales,
                start=True,
                stop=True,
            )

        h_bf = []
        for c in range(TILES):
            tok = slice(P * c, P * (c + 1))
            h_ps = psum.tile([P, PACK, P], F32, name="h_ps%d" % c, tag="bank%d" % c)
            for t in range(PACK):
                cols = slice(P * t, P * (t + 1))
                product(h_ps[:, t, :], w_codes[:, cols], w_scales[:, cols], xw[:, tok], xs[:, tok])
            rounded = sb([P, P, PACK], BF16, "h_bf%d" % c)
            nc.scalar.copy(rounded[:], h_ps[:].rearrange("p t n -> p n t"))
            h_bf.append(rounded)

        es = gather(es_tab, coh_sb, U, U8, "es")
        ew = gather(ew_tab, coh_sb, U, U32, "ew")

        h_codes = sb([P, S], U32, "h_codes", "ew_tab")
        h_scales = sb([P, S], U8, "h_scales")
        z_ps = []
        for c in range(TILES):
            tok = slice(P * c, P * (c + 1))
            nc.vector.quantize_mx(out=h_codes[:, tok].bitcast(FP8X4), scales=h_scales[:, tok], in_=h_bf[c][:].rearrange("p n t -> p (n t)"))
            z = psum.tile([P, U], F32, name="z_ps%d" % c, tag="bank%d" % (TILES + c))
            product(z[:], h_codes[:, tok], h_scales[:, tok], ew[:], es[:])
            z_ps.append(z)

        dw = gather(dw_tab, spk_sb, V, U32, "dw", "h_bf1")

        neg_mean = sb([P, TILES], F32, "neg_mean")
        gain = sb([P, TILES], F32, "gain")
        shift = sb([P, TILES], F32, "shift")
        spill = sb([P, U], BF16, "spill")
        squares = sb([P, 2], F32, "squares")
        quarter = sb([P, 2], F32, "quarter")
        for c in range(2):
            own = slice(c, c + 1)
            nc.scalar.activation(spill[:], z_ps[c][:], ACT.Copy, scale=-1.0 / U, accum_out=neg_mean[:, own])
            nc.scalar.activation(spill[:], z_ps[c][:], ACT.Square, bias=neg_mean[:, own], accum_out=squares[:, own])
            nc.scalar.activation(quarter[:, own], squares[:, own], ACT.Copy, scale=0.25 / U, bias=0.25 * EPS)
        stats = sb([P, 2, 6], F32, "stats", "dw_tab")
        mean_var = sb([P, 2, 2], F32, "mean_var")
        for g in range(2):
            nc.vector.bn_stats(stats[:, g, :], z_ps[2 + g][:])
        for g in range(2):
            nc.vector.bn_aggr(mean_var[:, g, :], stats[:, g, :])
        quarter_late = sb([P, 2], F32, "quarter_late")
        nc.scalar.activation(neg_mean[:, 2:4], mean_var[:, :, 0], ACT.Copy, scale=-1.0)

        ds = gather(ds_tab, spk_sb, V, U8, "ds")
        ms_spk = gather(ms_tab, spk_sb, V, F32, "ms_spk")

        nc.gpsimd.tensor_tensor(gain[:, 0:1], quarter[:, 0:1], minus_half[:, 0:1], ALU.pow)
        nc.gpsimd.tensor_scalar(quarter_late[:], mean_var[:, :, 1], 0.25, 0.25 * EPS, ALU.mult, ALU.add)
        nc.gpsimd.tensor_tensor(gain[:, 2:4], quarter_late[:], minus_half[:], ALU.pow)
        nc.gpsimd.tensor_tensor(gain[:, 1:2], quarter[:, 1:2], minus_half[:, 0:1], ALU.pow)

        for c in (0, 2, 3, 1):
            tok = slice(P * c, P * (c + 1))
            own = slice(c, c + 1)
            y = psum.tile([P, V], F32, name="y_ps%d" % c, tag="bank%d" % c)
            product(y[:], h_codes[:, tok], h_scales[:, tok], dw[:], ds[:])
            nc.scalar.activation(shift[:, own], neg_mean[:, own], ACT.Copy, scale=gain[:, own])
            pieces = 2 if c == LAST else 1
            for k in range(pieces):
                cols = slice(V // pieces * k, V // pieces * (k + 1))
                logit = sb([P, V // pieces], F32, "logit%d_%d" % (c, k))
                nc.vector.scalar_tensor_tensor(logit[:], y[:, cols], gain[:, own], ms_spk[:, cols], ALU.mult, ALU.subtract)
                prob = sb([P, V // pieces], F32, "prob%d_%d" % (c, k))
                nc.scalar.activation(prob[:], logit[:], ACT.Sigmoid, bias=shift[:, own])
                nc.sync.dma_start(out[tok, cols], prob[:])
